import numpy as np
import ml_dtypes


def mxq(x, axis, fmt="e4m3"):
    dtype, down = {"e4m3": (ml_dtypes.float8_e4m3fn, 7), "e5m2": (ml_dtypes.float8_e5m2, 14)}[fmt]
    v = np.moveaxis(np.asarray(x, np.float32).astype(ml_dtypes.bfloat16).astype(np.float64), axis, -1)
    blocks = v.reshape(v.shape[:-1] + (-1, 32))
    amax = np.abs(blocks).max(-1, keepdims=True)
    byte = np.maximum(np.where(amax > 0, np.frexp(amax)[1] - 1 + 127, 0) - down, 1)
    scale = np.exp2(byte - 127.0)
    codes = (blocks / scale).astype(np.float32).astype(dtype).astype(np.float64)
    return np.moveaxis((codes * scale).reshape(v.shape), -1, axis)


WIDE = False


def mx_kscale(k):
    if not WIDE:
        return np.ones(k)
    levels = np.array([10, -10, 5, -5, 0])
    if k % 512:
        return np.exp2(np.random.permutation(np.resize(levels, k // 32))).repeat(32)
    a = np.empty((k // 512, 16))
    for p in range(k // 512):
        a[p, :8] = np.random.permutation(np.resize(levels, 8))
        for g in range(8):
            far = levels[np.abs(levels - a[p, g]) >= 10]
            a[p, g + 8] = far[np.random.randint(len(far))]
    return np.exp2(a.ravel()).repeat(32)


BF16 = ml_dtypes.bfloat16


def bf(x):
    return np.asarray(x, np.float32).astype(BF16)


def f64(x):
    return np.asarray(x).astype(np.float64)


E2M1 = np.array([0.0, 0.5, 1.0, 1.5, 2.0, 3.0, 4.0, 6.0, -0.0, -0.5, -1.0, -1.5, -2.0, -3.0, -4.0, -6.0])


def pack_weight(w, fmt):
    k, n = w.shape
    w = f64(bf(w)).reshape(k // 32, 32, n)
    amax = np.abs(w).max(1)
    if fmt == "e4m3":
        byte = np.frexp(amax)[1] - 1 + 127 - 7
    else:
        mant, ex = np.frexp(amax / 6.0)
        byte = np.where(mant > 0.5, ex, ex - 1) + 127
    byte = np.clip(np.where(amax > 0, byte, 1), 1, 254)
    scaled = (w * np.exp2(127.0 - byte)[:, None, :]).reshape(k, n).astype(np.float32)
    by_word = np.ascontiguousarray(scaled.reshape(k // 512, 128, 4, n).transpose(0, 1, 3, 2))
    if fmt == "e4m3":
        words = by_word.astype(ml_dtypes.float8_e4m3fn).view(np.uint8)
    else:
        c = by_word.astype(ml_dtypes.float4_e2m1fn).view(np.uint8) & 0xF
        words = c[..., 0::2] | (c[..., 1::2] << 4)
    return np.ascontiguousarray(words), np.ascontiguousarray(byte.astype(np.uint8).reshape(k // 512, 16, n))


def unpack_weight(words, scales, fmt):
    g, p, n, _ = words.shape
    if fmt == "e4m3":
        vals = np.ascontiguousarray(words).view(ml_dtypes.float8_e4m3fn).astype(np.float64)
    else:
        nib = np.empty((g, p, n, 4), np.uint8)
        nib[..., 0::2] = words & 0xF
        nib[..., 1::2] = words >> 4
        vals = E2M1[nib]
    vals = vals * np.repeat(np.exp2(scales.astype(np.float64) - 127.0), 8, axis=1)[..., None]
    return vals.transpose(0, 1, 3, 2).reshape(g * 512, n)

def planes(Y):
    n, m = Y.shape
    b = f64(bf(Y)).reshape(n // 32, 32, m)
    amax = np.abs(b).max(1)
    byte = np.clip(np.where(amax > 0, np.frexp(amax)[1] - 1 + 127 - 7, 1), 1, 254)
    codes = (b * np.exp2(127.0 - byte)[:, None, :]).reshape(n, m).astype(np.float32).astype(ml_dtypes.float8_e4m3fn).view(np.uint8)
    words = codes.reshape(n // 512, 128, 4, m).transpose(0, 1, 3, 2)
    return np.ascontiguousarray(words), np.ascontiguousarray(byte.astype(np.uint8).reshape(n // 512, 16, m))


B, N, D, E, F = 2, 512, 1024, 1024, 1024


def setup_inputs():
    s, t = mx_kscale(D), mx_kscale(E)
    x = bf(np.random.standard_normal((B, N, D)) * s)
    wi = bf(np.random.standard_normal(D) * 2.0 / np.sqrt(D) / s)
    wk_words, wk_scales = pack_weight(np.random.standard_normal((D, E)) * 2.0 / np.sqrt(D) / s[:, None], "e4m3")
    wv_words, wv_scales = pack_weight(np.random.standard_normal((D, E)) / np.sqrt(D) / s[:, None] * t, "e4m3")
    wo_words, wo_scales = pack_weight(np.random.standard_normal((E, F)) / np.sqrt(E) / t[:, None], "e4m3")
    return {"x": x,
            "wi": wi,
            "wk_words": wk_words, "wk_scales": wk_scales,
            "wv_words": wv_words, "wv_scales": wv_scales,
            "wo_words": wo_words, "wo_scales": wo_scales,
            "bo": bf(np.random.standard_normal(F) * 0.1)}


def context_scores(x, wi):
    a = np.sum(x * wi, axis=-1)
    e = np.exp(a - a.max(axis=1, keepdims=True))
    return e / e.sum(axis=1, keepdims=True)


def core(x, wi, wk_words, wk_scales, wv_words, wv_scales, wo_words, wo_scales, bo):
    xf = f64(x)
    c = context_scores(xf, f64(wi))
    xq = mxq(xf, 2, "e4m3")
    k = xq @ unpack_weight(wk_words, wk_scales, "e4m3")
    cv = np.sum(c[:, :, None] * k, axis=1)
    v = np.maximum(xq @ unpack_weight(wv_words, wv_scales, "e4m3"), 0.0)
    z = v * cv[:, None, :]
    return (mxq(z, 2, "e4m3") @ unpack_weight(wo_words, wo_scales, "e4m3")) + f64(bo)


def reference(x, wi, wk_words, wk_scales, wv_words, wv_scales, wo_words, wo_scales, bo):
    R_out = core(x, wi, wk_words, wk_scales, wv_words, wv_scales, wo_words, wo_scales, bo)
    words, scales = planes(np.moveaxis(R_out, 2, 0).reshape(1024, -1))
    return R_out, words, scales

@@ -1,0 +1,488 @@
+from contextlib import ExitStack
+
+import concourse.mybir as mybir
+from concourse.masks import make_identity
+
+F32 = mybir.dt.float32
+BF16 = mybir.dt.bfloat16
+I32 = mybir.dt.int32
+U8 = mybir.dt.uint8
+FP8X4 = mybir.dt.float8_e4m3fn_x4
+ALU = mybir.AluOpType
+ACT = mybir.ActivationFunctionType
+AX = mybir.AxisListType
+
+B, N, D = 2, 512, 1024
+P = 128
+G = 2
+NT = 4
+FLOPS = 3 * 2 * B * N * D * D
+
+
+def tile_mobilevitv2separablecontextgate_x2_kernel(
+    tc, x, wi, wk_words, wk_scales, wv_words, wv_scales, wo_words, wo_scales, bo, out_0, out_1, out_2
+):
+    nc = tc.nc
+    with ExitStack() as ctx:
+        keep = ctx.enter_context(tc.tile_pool(name="keep", bufs=1))
+        work = ctx.enter_context(tc.tile_pool(name="work", bufs=3))
+        psum = ctx.enter_context(tc.psum_pool(name="psum", bufs=1))
+        ctx.enter_context(tc.manual_schedule())
+
+        def sb(name, shape, dtype):
+            return keep.tile(shape, dtype, name=name, align_bytes=64)
+
+        ident = sb("ident", [P, P], F32)
+        rsel = sb("rsel", [P, 32], F32)
+        bsel = sb("bsel", [P, 4, 32], F32)
+        mask_t = sb("mask_t", [P, 4], F32)
+        mask_q = sb("mask_q", [P, 4], F32)
+        wi_sb = sb("wi_sb", [P, G, 4], BF16)
+        bo_sb = sb("bo_sb", [P, D], BF16)
+        wk_sb = sb("wk_sb", [P, G, D], I32)
+        wv_in = sb("wv_in", [P, G, D], I32)
+        wv_sb = sb("wv_sb", [P, G, D], I32)
+        wo_sb = sb("wo_sb", [P, G, D], I32)
+        wk_s = sb("wk_s", [P, D], U8)
+        wvs_in = sb("wvs_in", [P, D], U8)
+        wv_s = sb("wv_s", [P, D], U8)
+        wo_s = sb("wo_s", [P, D], U8)
+        x_sb = [sb("x_sb_%d" % b, [P, NT, D], BF16) for b in range(B)]
+        xt = [sb("xt_%d" % b, [P, G, N, 4], BF16) for b in range(B)]
+        xq = [sb("xq_%d" % b, [P, G, N], I32) for b in range(B)]
+        xs = [sb("xs_%d" % b, [P, G, N], U8) for b in range(B)]
+        escore = [sb("escore_%d" % b, [P, N], F32) for b in range(B)]
+        amax = [sb("amax_%d" % b, [P, 1], F32) for b in range(B)]
+        esum = [sb("esum_%d" % b, [P, 1], F32) for b in range(B)]
+        rsum = [sb("rsum_%d" % b, [P, 1], F32) for b in range(B)]
+        cvraw = [sb("cvraw_%d" % b, [P, 8], F32) for b in range(B)]
+        cvspread = [sb("cvspread_%d" % b, [P, 4, 8], F32) for b in range(B)]
+        cvpick = [sb("cvpick_%d" % b, [P, 8, 4], F32) for b in range(B)]
+        cvz = [sb("cvz_%d" % b, [P, 4, G], F32) for b in range(B)]
+        zq = [sb("zq_%d" % b, [P, NT, G, P], I32) for b in range(B)]
+        zs = [sb("zs_%d" % b, [P, NT, G, P], U8) for b in range(B)]
+        yt = [sb("yt_%d" % b, [P, G, N, 4], BF16) for b in range(B)]
+        yq = [sb("yq_%d" % b, [P, G, N], I32) for b in range(B)]
+        ys = [sb("ys_%d" % b, [P, N], U8) for b in range(B)]
+
+        def words(dram, g):
+            return dram[g].rearrange("p n t -> p (n t)").bitcast(I32)
+
+        def load_scales(engine, tile, dram):
+            for q in range(4):
+                engine.dma_start(
+                    out=tile[32 * q : 32 * q + 8, :].bitcast(I32),
+                    in_=dram[:, 4 * q : 4 * q + 4, :].bitcast(I32),
+                )
+
+        def load_x(b, lo, hi):
+            nc.sync.dma_start(
+                out=x_sb[b][:, lo:hi, :], in_=x[b, P * lo : P * hi, :].rearrange("(i p) d -> p i d", p=P)
+            )
+
+        tr_tiles = {}
+
+        def x_transposes(b, i):
+            bank = psum.tile([P, 4, P], F32, name="trbank", tag="tr", bufs=2)
+            w = x_sb[b][:, i, :].bitcast(F32)
+            for g in range(G):
+                for u in range(2):
+                    nc.tensor.transpose(
+                        bank[:, 2 * g + u, :], w[:, 256 * g + u : 256 * (g + 1) : 2], ident[:]
+                    )
+            tr_tiles[("x", b, i)] = bank
+
+        def evacuate(engine, bank, dst, i):
+            out = dst[:, :, P * i : P * (i + 1), :].bitcast(F32)
+            src = bank[:].rearrange("p (g u) r -> p g r u", u=2)
+            if engine is nc.vector:
+                engine.tensor_copy(out=out, in_=src)
+            else:
+                engine.copy(out=out, in_=src)
+
+        xw = sb("xw", [P, NT, 4, P], F32)
+
+        def x_reorder(i):
+            nc.scalar.copy(
+                out=xw[:, i].rearrange("n (g u) p -> n g u p", u=2),
+                in_=x_sb[1][:, i, :].bitcast(F32).rearrange("n (g p u) -> n g u p", g=2, u=2),
+            )
+
+        def x_transposes_reordered(i):
+            bank = psum.tile([P, 4, P], F32, name="trbank", tag="tr", bufs=2)
+            for k in range(4):
+                nc.tensor.transpose(bank[:, k, :], xw[:, i, k, :], ident[:])
+            tr_tiles[("x", 1, i)] = bank
+
+        def x_copy(engine, b, i):
+            evacuate(engine, tr_tiles.pop(("x", b, i)), xt[b], i)
+
+        def quantize_tokens(src, codes, scales, g, lo, hi, packed):
+            nc.vector.quantize_mx(
+                out=codes[:, g, lo:hi].bitcast(FP8X4),
+                scales=scales[4 * g : P, lo:hi] if packed else scales[:, g, lo:hi],
+                in_=src[:, g, lo:hi, :].rearrange("p n t -> p (n t)"),
+            )
+
+        def x_quant(b, lo, hi):
+            for g in range(G):
+                quantize_tokens(xt[b], xq[b], xs[b], g, lo, hi, False)
+
+        a_tiles = {}
+
+        def a_matmuls(b, lo, hi):
+            if lo == 0:
+                a_tiles[b] = psum.tile([P, N], F32, name="abank", tag="y", bufs=2)
+            bank = a_tiles[b]
+            for k in range(8):
+                g, t = divmod(k, 4)
+                nc.tensor.matmul(
+                    bank[:, lo:hi],
+                    lhsT=wi_sb[:, g, t : t + 1].to_broadcast([P, P]),
+                    rhs=xt[b][:, g, lo:hi, t],
+                    start=(k == 0),
+                    stop=(k == 7),
+                )
+
+        def a_softmax(b):
+            bank = a_tiles.pop(b)
+            nc.vector.reduce_max(out=amax[b][:], in_=bank[:], axis=AX.X)
+            nc.vector.tensor_scalar(out=amax[b][:], in0=amax[b][:], scalar1=-1.0, scalar2=None, op0=ALU.mult)
+            nc.scalar.activation(
+                out=escore[b][:], in_=bank[:], func=ACT.Exp, bias=amax[b][:], scale=1.0, accum_out=esum[b][:]
+            )
+
+        k_tiles = {}
+
+        def k_matmuls(b, m):
+            bank = psum.tile([P, N], F32, name="kbank", tag="mm", bufs=4)
+            cols = slice(P * m, P * (m + 1))
+            for g in range(G):
+                nc.tensor.matmul_mx(
+                    out=bank[:],
+                    lhsT=wk_sb[:, g, cols].bitcast(FP8X4),
+                    lhsT_scale=wk_s[4 * g : P, cols],
+                    rhs=xq[b][:, g, :].bitcast(FP8X4),
+                    rhs_scale=xs[b][:, g, :],
+                    start=(g == 0),
+                    stop=(g == 1),
+                )
+            k_tiles[(b, m)] = bank
+
+        def k_pool(b, m):
+            product = work.tile([P, N], BF16, name="product", align_bytes=64)
+            nc.vector.scalar_tensor_tensor(
+                out=product[:],
+                in0=k_tiles.pop((b, m))[:],
+                scalar=1.0,
+                in1=escore[b][:],
+                op0=ALU.mult,
+                op1=ALU.mult,
+                accum_out=cvraw[b][:, m : m + 1],
+            )
+
+        sh_tiles = {}
+
+        def cv_spread(b):
+            nc.vector.reciprocal(out=rsum[b][:], in_=esum[b][:])
+            nc.vector.tensor_tensor(
+                out=cvspread[b][:],
+                in0=cvraw[b][:].unsqueeze(1).to_broadcast([P, 4, 8]),
+                in1=mask_t[:].unsqueeze(2).to_broadcast([P, 4, 8]),
+                op=ALU.mult,
+            )
+
+        def cv_move(b):
+            bank = psum.tile([P, 8, 4], F32, name="shbank", tag="y", bufs=2)
+            nc.tensor.matmul(
+                bank[:].rearrange("p a q -> p (a q)"),
+                lhsT=bsel[:].rearrange("p q j -> p (q j)"),
+                rhs=cvspread[b][:].rearrange("p t m -> p (t m)"),
+                start=True,
+                stop=True,
+            )
+            sh_tiles[b] = bank
+
+        def cv_pick(b):
+            nc.vector.scalar_tensor_tensor(
+                out=cvpick[b][:],
+                in0=sh_tiles.pop(b)[:],
+                scalar=rsum[b][:],
+                in1=mask_q[:].unsqueeze(1).to_broadcast([P, 8, 4]),
+                op0=ALU.mult,
+                op1=ALU.mult,
+            )
+            nc.vector.reduce_sum(
+                out=cvz[b][:].rearrange("p t g -> p (t g)"), in_=cvpick[b][:], axis=AX.X
+            )
+
+        v_tiles = {}
+        z_tiles = {}
+
+        def v_matmuls(b, i, h):
+            bank = psum.tile([P, 4, P], F32, name="vbank", tag="mm", bufs=4)
+            for t in range(4):
+                cols = slice(512 * h + P * t, 512 * h + P * (t + 1))
+                for g in range(G):
+                    nc.tensor.matmul_mx(
+                        out=bank[:, t, :],
+                        lhsT=wv_sb[:, g, cols].bitcast(FP8X4),
+                        lhsT_scale=wv_s[4 * g : P, cols],
+                        rhs=xq[b][:, g, P * i : P * (i + 1)].bitcast(FP8X4),
+                        rhs_scale=xs[b][:, g, P * i : P * (i + 1)],
+                        start=(g == 0),
+                        stop=(g == 1),
+                    )
+            v_tiles[(b, i, h)] = bank
+
+        def v_gate(b, i, h):
+            if h == 0:
+                z_tiles[(b, i)] = work.tile([P, G, P, 4], BF16, name="z", align_bytes=64)
+            nc.vector.scalar_tensor_tensor(
+                out=z_tiles[(b, i)][:, h],
+                in0=v_tiles.pop((b, i, h))[:].rearrange("p t n -> p n t"),
+                scalar=0.0,
+                in1=cvz[b][:, :, h].unsqueeze(1).to_broadcast([P, P, 4]),
+                op0=ALU.max,
+                op1=ALU.mult,
+            )
+
+        def z_quant(b, i):
+            nc.vector.quantize_mx(
+                out=zq[b][:, i].rearrange("p g n -> p (g n)").bitcast(FP8X4),
+                scales=zs[b][:, i].rearrange("p g n -> p (g n)"),
+                in_=z_tiles.pop((b, i))[:].rearrange("p g n t -> p (g n t)"),
+            )
+
+        y_banks = {}
+        y_rows = {}
+        y_half = {}
+
+        def y_matmuls(b, i, f):
+            bank = psum.tile([P, 512], F32, name="ybank", tag="y", bufs=2)
+            cols = slice(512 * f, 512 * (f + 1))
+            for g in range(G):
+                nc.tensor.matmul_mx(
+                    out=bank[:],
+                    lhsT=zq[b][:, i, g, :].bitcast(FP8X4),
+                    lhsT_scale=zs[b][:, i, g, :],
+                    rhs=wo_sb[:, g, cols].bitcast(FP8X4),
+                    rhs_scale=wo_s[4 * g : P, cols],
+                    start=(g == 0),
+                    stop=(g == 1),
+                )
+            y_banks[(b, i, f)] = bank
+
+        def y_add(b, i, f):
+            if f == 0:
+                y_rows[(b, i)] = work.tile([P, D], F32, name="yrow", align_bytes=64)
+            cols = slice(512 * f, 512 * (f + 1))
+            nc.vector.tensor_tensor(
+                out=y_rows[(b, i)][:, cols], in0=y_banks.pop((b, i, f))[:], in1=bo_sb[:, cols], op=ALU.add
+            )
+
+        y_raw = {}
+
+        def y_raw_copy(b, i, f):
+            y_raw[(b, i, f)] = work.tile([P, 512], F32, name="yraw", align_bytes=64)
+            nc.scalar.copy(out=y_raw[(b, i, f)][:], in_=y_banks.pop((b, i, f))[:])
+
+        def y_add_pool(b, i, f):
+            if f == 0:
+                y_rows[(b, i)] = work.tile([P, D], F32, name="yrow", align_bytes=64)
+            cols = slice(512 * f, 512 * (f + 1))
+            nc.gpsimd.tensor_tensor(
+                out=y_rows[(b, i)][:, cols], in0=y_raw.pop((b, i, f))[:], in1=bo_sb[:, cols], op=ALU.add
+            )
+
+        def y_store(b, i):
+            nc.sync.dma_start(out=out_0[b, P * i : P * (i + 1), :], in_=y_rows[(b, i)][:])
+
+        def y_round(engine, b, i, f):
+            if f == 0:
+                y_half[(b, i)] = work.tile([P, G, 2, P, 2], BF16, name="yhalf", align_bytes=64)
+            src = y_rows[(b, i)][:, 512 * f : 512 * (f + 1)].rearrange("n (p u e) -> n u p e", u=2, e=2)
+            if engine is nc.vector:
+                engine.tensor_copy(out=y_half[(b, i)][:, f], in_=src)
+            else:
+                engine.copy(out=y_half[(b, i)][:, f], in_=src)
+
+        def y_transposes(b, i):
+            bank = psum.tile([P, 4, P], F32, name="trbank", tag="tr", bufs=2)
+            w = y_half.pop((b, i))[:].rearrange("n g u p e -> n (g u p e)").bitcast(F32)
+            for k in range(4):
+                nc.tensor.transpose(bank[:, k, :], w[:, P * k : P * (k + 1)], ident[:])
+            tr_tiles[("y", b, i)] = bank
+
+        def y_copy(engine, b, i):
+            evacuate(engine, tr_tiles.pop(("y", b, i)), yt[b], i)
+
+        def y_quant(b, lo, hi, g):
+            quantize_tokens(yt[b], yq[b], ys[b], g, lo, hi, True)
+
+        def plane_store(b, lo, hi):
+            for g in range(G):
+                nc.sync.dma_start(
+                    out=words(out_1, g)[:, N * b + lo : N * b + hi], in_=yq[b][:, g, lo:hi]
+                )
+            for q in range(4):
+                nc.sync.dma_start(
+                    out=out_2[:, 4 * q : 4 * q + 4, N * b + lo : N * b + hi].bitcast(I32),
+                    in_=ys[b][32 * q : 32 * q + 8, lo:hi].bitcast(I32),
+                )
+
+        def permute_wv(g):
+            nc.vector.tensor_copy(
+                out=wv_sb[:, g, :].rearrange("p (h t j) -> p h t j", h=2, t=4),
+                in_=wv_in[:, g, :].rearrange("p (h j t) -> p h t j", h=2, t=4),
+            )
+
+        def permute_wv_scales():
+            nc.vector.tensor_copy(
+                out=wv_s[:].rearrange("p (h t j) -> p h t j", h=2, t=4),
+                in_=wvs_in[:].rearrange("p (h j t) -> p h t j", h=2, t=4),
+            )
+
+        def load_wk(lo, hi):
+            nc.sync.dma_start(
+                out=wk_sb[:, :, lo:hi],
+                in_=wk_words.rearrange("g p n t -> p g (n t)").bitcast(I32)[:, :, lo:hi],
+            )
+
+        for i in range(NT):
+            load_x(0, i, i + 1)
+        nc.scalar.dma_start(out=wi_sb[:], in_=wi.rearrange("(g p t) -> p g t", p=P, t=4))
+        for tile in (wk_s, wvs_in, wo_s):
+            nc.vector.memset(tile[:].bitcast(I32), 0)
+        make_identity(nc, ident[:])
+        load_scales(nc.gpsimd, wk_s, wk_scales)
+        load_scales(nc.gpsimd, wvs_in, wv_scales)
+        load_scales(nc.gpsimd, wo_s, wo_scales)
+        load_wk(0, 512)
+        for g in range(G):
+            nc.sync.dma_start(out=wv_in[:, g, :], in_=words(wv_words, g))
+        load_wk(512, D)
+        load_x(1, 0, 2)
+        load_x(1, 2, 4)
+        for g in range(G):
+            nc.sync.dma_start(out=wo_sb[:, g, :], in_=words(wo_words, g))
+        nc.sync.dma_start(out=bo_sb[:], in_=bo.partition_broadcast(P))
+
+        nc.vector.reduce_sum(out=rsel[:], in_=ident[:].rearrange("p (j t) -> p j t", t=4), axis=AX.X)
+        nc.vector.reduce_sum(out=mask_t[:], in_=ident[:].rearrange("p (j t) -> p t j", t=4), axis=AX.X)
+        nc.vector.reduce_sum(out=mask_q[:], in_=ident[:].rearrange("p (q j) -> p q j", q=4), axis=AX.X)
+        nc.vector.tensor_copy(out=bsel[:], in_=rsel[:].unsqueeze(1).to_broadcast([P, 4, 32]))
+
+        for i in range(NT):
+            x_transposes(0, i)
+            x_copy(nc.vector if i % 2 else nc.scalar, 0, i)
+            if i > 0:
+                a_matmuls(0, P * (i - 1), P * i)
+                x_quant(0, P * (i - 1), P * i)
+        a_matmuls(0, P * (NT - 1), N)
+        x_quant(0, P * (NT - 1), N)
+        permute_wv(0)
+        a_softmax(0)
+        permute_wv(1)
+        permute_wv_scales()
+        for i in range(NT):
+            x_reorder(i)
+        for m in range(8):
+            k_matmuls(0, m)
+            k_pool(0, m)
+            if m % 2:
+                x_transposes_reordered(m // 2)
+                x_copy(nc.scalar, 1, m // 2)
+        cv_spread(0)
+        cv_move(0)
+        x_quant(1, 0, N)
+        cv_pick(0)
+        for i in range(NT):
+            for h in range(G):
+                v_matmuls(0, i, h)
+                v_gate(0, i, h)
+            if i > 0:
+                z_quant(0, i - 1)
+            a_matmuls(1, P * i, P * (i + 1))
+        a_softmax(1)
+        def y_front(b, i, f, pool):
+            y_matmuls(b, i, f)
+            if pool:
+                y_raw_copy(b, i, f)
+                y_add_pool(b, i, f)
+            else:
+                y_add(b, i, f)
+
+        y0 = [(0, i, f) for i in range(NT) for f in range(G)]
+        rounds = []
+        turns = []
+
+        def y_turn():
+            i = turns.pop(0)
+            y_transposes(0, i)
+            y_copy(nc.scalar, 0, i)
+
+        def y0_step(pool):
+            if y0:
+                b, i, f = y0.pop(0)
+                y_front(b, i, f, pool)
+                rounds.append((b, i, f))
+            if len(rounds) > 2:
+                b, i, f = rounds.pop(0)
+                y_round(nc.scalar, b, i, f)
+                if f == 1:
+                    y_store(b, i)
+                    turns.append(i)
+            elif turns:
+                y_turn()
+
+        for m in range(8):
+            k_matmuls(1, m)
+            k_pool(1, m)
+            if m == 1:
+                z_quant(0, NT - 1)
+            if m in (2, 4, 6):
+                y0_step(m in (2, 6))
+        cv_spread(1)
+        y0_step(True)
+        y0_step(False)
+        cv_move(1)
+        cv_pick(1)
+        for i in range(NT):
+            for h in range(G):
+                v_matmuls(1, i, h)
+                v_gate(1, i, h)
+                y0_step((i + h) % 2 == 0)
+                if turns and h == 1:
+                    y_turn()
+            if i > 0:
+                z_quant(1, i - 1)
+        for b, i, f in rounds:
+            y_round(nc.scalar, b, i, f)
+        y_store(0, NT - 1)
+        turns.append(NT - 1)
+        z_quant(1, NT - 1)
+        for i in range(NT):
+            for f in range(G):
+                y_front(1, i, f, False)
+                y_round(nc.scalar, 1, i, f)
+                if turns:
+                    y_turn()
+            y_store(1, i)
+            if i == 1:
+                y_quant(0, 0, N, 0)
+            if i == 2:
+                y_quant(0, 0, N, 1)
+                plane_store(0, 0, N)
+            if i > 0:
+                y_transposes(1, i - 1)
+                y_copy(nc.scalar, 1, i - 1)
+            if i == 3:
+                for g in range(G):
+                    y_quant(1, 0, 256, g)
+                plane_store(1, 0, 256)
+        y_transposes(1, NT - 1)
+        y_copy(nc.scalar, 1, NT - 1)
+        for g in range(G):
+            y_quant(1, 256, N, g)
+        plane_store(1, 256, N)

@@ -38,6 +38,7 @@ def tile_mobilevitv2separablecontextgate_x2_kernel(
         mask_t = sb("mask_t", [P, 4], F32)
         mask_q = sb("mask_q", [P, 4], F32)
         wi_sb = sb("wi_sb", [P, G, 4], BF16)
+        wi_neg = sb("wi_neg", [P, G, 4], BF16)
         bo_sb = sb("bo_sb", [P, D], BF16)
         wk_sb = sb("wk_sb", [P, G, D], I32)
         wv_in = sb("wv_in", [P, G, D], I32)
@@ -83,7 +84,10 @@ def tile_mobilevitv2separablecontextgate_x2_kernel(
         tr_tiles = {}
 
         def x_transposes(b, i):
-            bank = psum.tile([P, 4, P], F32, name="trbank", tag="tr", bufs=2)
+            if i < 2:
+                bank = psum.tile([P, 4, P], F32, name="trbank", tag="tr", bufs=2)
+            else:
+                bank = psum.tile([P, 4, P], F32, name="trbank", tag="mm", bufs=4)
             w = x_sb[b][:, i, :].bitcast(F32)
             for g in range(G):
                 for u in range(2):
@@ -138,7 +142,7 @@ def tile_mobilevitv2separablecontextgate_x2_kernel(
                 g, t = divmod(k, 4)
                 nc.tensor.matmul(
                     bank[:, lo:hi],
-                    lhsT=wi_sb[:, g, t : t + 1].to_broadcast([P, P]),
+                    lhsT=wi_neg[:, g, t : t + 1].to_broadcast([P, P]),
                     rhs=xt[b][:, g, lo:hi, t],
                     start=(k == 0),
                     stop=(k == 7),
@@ -146,10 +150,9 @@ def tile_mobilevitv2separablecontextgate_x2_kernel(
 
         def a_softmax(b):
             bank = a_tiles.pop(b)
-            nc.vector.reduce_max(out=amax[b][:], in_=bank[:], axis=AX.X)
-            nc.vector.tensor_scalar(out=amax[b][:], in0=amax[b][:], scalar1=-1.0, scalar2=None, op0=ALU.mult)
+            nc.vector.tensor_reduce(out=amax[b][:], in_=bank[:], axis=AX.X, op=ALU.min)
             nc.scalar.activation(
-                out=escore[b][:], in_=bank[:], func=ACT.Exp, bias=amax[b][:], scale=1.0, accum_out=esum[b][:]
+                out=escore[b][:], in_=bank[:], func=ACT.Exp, bias=amax[b][:], scale=-1.0, accum_out=esum[b][:]
             )
 
         k_tiles = {}
@@ -247,6 +250,26 @@ def tile_mobilevitv2separablecontextgate_x2_kernel(
                 op1=ALU.mult,
             )
 
+        def v_gate_pool(b, i, h):
+            if h == 0:
+                z_tiles[(b, i)] = work.tile([P, G, P, 4], BF16, name="z", align_bytes=64)
+            vrelu = work.tile([P, P, 4], F32, name="vrelu", align_bytes=64)
+            nc.scalar.activation(
+                out=vrelu[:], in_=v_tiles.pop((b, i, h))[:].rearrange("p t n -> p n t"), func=ACT.Relu
+            )
+            nc.gpsimd.tensor_tensor(
+                out=z_tiles[(b, i)][:, h],
+                in0=vrelu[:],
+                in1=cvz[b][:, :, h].unsqueeze(1).to_broadcast([P, P, 4]),
+                op=ALU.mult,
+            )
+
+        def gate(b, i, h):
+            if (b, i, h) in ((0, 0, 0), (0, 2, 0), (0, 3, 1)):
+                v_gate_pool(b, i, h)
+            else:
+                v_gate(b, i, h)
+
         def z_quant(b, i):
             nc.vector.quantize_mx(
                 out=zq[b][:, i].rearrange("p g n -> p (g n)").bitcast(FP8X4),
@@ -259,7 +282,10 @@ def tile_mobilevitv2separablecontextgate_x2_kernel(
         y_half = {}
 
         def y_matmuls(b, i, f):
-            bank = psum.tile([P, 512], F32, name="ybank", tag="y", bufs=2)
+            if b == 0:
+                bank = psum.tile([P, 512], F32, name="ybank", tag="y", bufs=2)
+            else:
+                bank = psum.tile([P, 512], F32, name="ybank", tag="mm", bufs=4)
             cols = slice(512 * f, 512 * (f + 1))
             for g in range(G):
                 nc.tensor.matmul_mx(
@@ -302,7 +328,11 @@ def tile_mobilevitv2separablecontextgate_x2_kernel(
             if f == 0:
                 y_half[(b, i)] = work.tile([P, G, 2, P, 2], BF16, name="yhalf", align_bytes=64)
             src = y_rows[(b, i)][:, 512 * f : 512 * (f + 1)].rearrange("n (p u e) -> n u p e", u=2, e=2)
-            if engine is nc.vector:
+            if engine is nc.gpsimd:
+                engine.tensor_scalar(
+                    out=y_half[(b, i)][:, f], in0=src, scalar1=1.0, scalar2=0.0, op0=ALU.mult, op1=ALU.add
+                )
+            elif engine is nc.vector:
                 engine.tensor_copy(out=y_half[(b, i)][:, f], in_=src)
             else:
                 engine.copy(out=y_half[(b, i)][:, f], in_=src)
@@ -314,19 +344,52 @@ def tile_mobilevitv2separablecontextgate_x2_kernel(
                 nc.tensor.transpose(bank[:, k, :], w[:, P * k : P * (k + 1)], ident[:])
             tr_tiles[("y", b, i)] = bank
 
+        def y_round_from_psum(b, i, f):
+            if f == 0:
+                y_half[(b, i)] = work.tile([P, G, 2, P, 2], BF16, name="yhalf", align_bytes=64)
+                y_rows[(b, i)] = work.tile([P, D], F32, name="yrow", align_bytes=64)
+            pairs = "n (p u e) -> n u p e"
+            cols = slice(512 * f, 512 * (f + 1))
+            nc.vector.tensor_tensor(
+                out=y_half[(b, i)][:, f],
+                in0=y_banks[(b, i, f)][:].rearrange(pairs, u=2, e=2),
+                in1=bo_sb[:, cols].rearrange(pairs, u=2, e=2),
+                op=ALU.add,
+            )
+
+        def y_add_last(b, i, f):
+            cols = slice(512 * f, 512 * (f + 1))
+            nc.vector.tensor_tensor(
+                out=y_rows[(b, i)][:, cols], in0=y_banks.pop((b, i, f))[:], in1=bo_sb[:, cols], op=ALU.add
+            )
+            nc.sync.dma_start(out=out_0[b, P * i : P * (i + 1), cols], in_=y_rows[(b, i)][:, cols])
+
+        def y_finish_half(engine, b, i, f):
+            bank = psum.tile([P, 2, P], F32, name="trbank", tag="tr", bufs=2)
+            w = y_half[(b, i)][:, f].rearrange("n u p e -> n (u p e)").bitcast(F32)
+            for u in range(2):
+                nc.tensor.transpose(bank[:, u, :], w[:, P * u : P * (u + 1)], ident[:])
+            out = yt[b][:, f, P * i : P * (i + 1), :].rearrange("p n t -> p (n t)").bitcast(F32)
+            out = out.rearrange("p (n u) -> p n u", u=2)
+            src = bank[:].rearrange("p u r -> p r u")
+            if engine is nc.vector:
+                engine.tensor_copy(out=out, in_=src)
+            else:
+                engine.copy(out=out, in_=src)
+
         def y_copy(engine, b, i):
             evacuate(engine, tr_tiles.pop(("y", b, i)), yt[b], i)
 
         def y_quant(b, lo, hi, g):
             quantize_tokens(yt[b], yq[b], ys[b], g, lo, hi, True)
 
-        def plane_store(b, lo, hi):
-            for g in range(G):
-                nc.sync.dma_start(
-                    out=words(out_1, g)[:, N * b + lo : N * b + hi], in_=yq[b][:, g, lo:hi]
-                )
+        def plane_store(engine, b, lo, hi):
+            nc.sync.dma_start(
+                out=out_1.rearrange("g p n t -> p g (n t)").bitcast(I32)[:, :, N * b + lo : N * b + hi],
+                in_=yq[b][:, :, lo:hi],
+            )
             for q in range(4):
-                nc.sync.dma_start(
+                (nc.sync if q % 2 else engine).dma_start(
                     out=out_2[:, 4 * q : 4 * q + 4, N * b + lo : N * b + hi].bitcast(I32),
                     in_=ys[b][32 * q : 32 * q + 8, lo:hi].bitcast(I32),
                 )
@@ -343,56 +406,65 @@ def tile_mobilevitv2separablecontextgate_x2_kernel(
                 in_=wvs_in[:].rearrange("p (h j t) -> p h t j", h=2, t=4),
             )
 
-        def load_wk(lo, hi):
+        def load_w(tile, dram, lo, hi):
             nc.sync.dma_start(
-                out=wk_sb[:, :, lo:hi],
-                in_=wk_words.rearrange("g p n t -> p g (n t)").bitcast(I32)[:, :, lo:hi],
+                out=tile[:, :, lo:hi],
+                in_=dram.rearrange("g p n t -> p g (n t)").bitcast(I32)[:, :, lo:hi],
             )
 
-        for i in range(NT):
-            load_x(0, i, i + 1)
-        nc.scalar.dma_start(out=wi_sb[:], in_=wi.rearrange("(g p t) -> p g t", p=P, t=4))
         for tile in (wk_s, wvs_in, wo_s):
             nc.vector.memset(tile[:].bitcast(I32), 0)
         make_identity(nc, ident[:])
-        load_scales(nc.gpsimd, wk_s, wk_scales)
-        load_scales(nc.gpsimd, wvs_in, wv_scales)
-        load_scales(nc.gpsimd, wo_s, wo_scales)
-        load_wk(0, 512)
-        for g in range(G):
-            nc.sync.dma_start(out=wv_in[:, g, :], in_=words(wv_words, g))
-        load_wk(512, D)
+        nc.scalar.dma_start(out=wi_sb[:], in_=wi.rearrange("(g p t) -> p g t", p=P, t=4))
+        load_scales(nc.scalar, wk_s, wk_scales)
+        for i in range(NT):
+            load_x(0, i, i + 1)
+        load_w(wk_sb, wk_words, 0, 512)
+        load_w(wv_in, wv_words, 0, D)
+        load_scales(nc.sync, wvs_in, wv_scales)
+        load_w(wk_sb, wk_words, 512, D)
         load_x(1, 0, 2)
         load_x(1, 2, 4)
-        for g in range(G):
-            nc.sync.dma_start(out=wo_sb[:, g, :], in_=words(wo_words, g))
+        load_w(wo_sb, wo_words, 0, D)
+        load_scales(nc.sync, wo_s, wo_scales)
         nc.sync.dma_start(out=bo_sb[:], in_=bo.partition_broadcast(P))
 
         nc.vector.reduce_sum(out=rsel[:], in_=ident[:].rearrange("p (j t) -> p j t", t=4), axis=AX.X)
         nc.vector.reduce_sum(out=mask_t[:], in_=ident[:].rearrange("p (j t) -> p t j", t=4), axis=AX.X)
         nc.vector.reduce_sum(out=mask_q[:], in_=ident[:].rearrange("p (q j) -> p q j", q=4), axis=AX.X)
+        nc.vector.tensor_scalar(out=wi_neg[:], in0=wi_sb[:], scalar1=-1.0, scalar2=None, op0=ALU.mult)
         nc.vector.tensor_copy(out=bsel[:], in_=rsel[:].unsqueeze(1).to_broadcast([P, 4, 32]))
 
+        for k in range(4):
+            bank = psum.tile([P, P], F32, name="warmbank", tag="tr", bufs=2)
+            nc.tensor.matmul(bank[:], lhsT=ident[:], rhs=ident[:], start=True, stop=True)
         for i in range(NT):
             x_transposes(0, i)
             x_copy(nc.vector if i % 2 else nc.scalar, 0, i)
-            if i > 0:
-                a_matmuls(0, P * (i - 1), P * i)
-                x_quant(0, P * (i - 1), P * i)
-        a_matmuls(0, P * (NT - 1), N)
-        x_quant(0, P * (NT - 1), N)
-        permute_wv(0)
+        a_matmuls(0, 0, 256)
+        a_matmuls(0, 256, N)
+        x_quant(0, 0, 256)
+        for i in (2, 3):
+            x_quant(0, P * i, P * (i + 1))
         a_softmax(0)
-        permute_wv(1)
-        permute_wv_scales()
-        for i in range(NT):
-            x_reorder(i)
+        permute_wv(0)
         for m in range(8):
             k_matmuls(0, m)
             k_pool(0, m)
-            if m % 2:
-                x_transposes_reordered(m // 2)
-                x_copy(nc.scalar, 1, m // 2)
+            if m == 1:
+                for i in range(NT):
+                    x_reorder(i)
+            if m == 2:
+                permute_wv(1)
+            if m == 4:
+                permute_wv_scales()
+            if m in (3, 5):
+                j = 2 * (3, 5).index(m)
+                for i in (j, j + 1):
+                    x_transposes_reordered(i)
+                for i in (j, j + 1):
+                    x_copy(nc.scalar, 1, i)
+        a_matmuls(1, 0, N)
         cv_spread(0)
         cv_move(0)
         x_quant(1, 0, N)
@@ -400,89 +472,99 @@ def tile_mobilevitv2separablecontextgate_x2_kernel(
         for i in range(NT):
             for h in range(G):
                 v_matmuls(0, i, h)
-                v_gate(0, i, h)
+                gate(0, i, h)
+                if i == 0 and h == 0:
+                    a_softmax(1)
             if i > 0:
                 z_quant(0, i - 1)
-            a_matmuls(1, P * i, P * (i + 1))
-        a_softmax(1)
-        def y_front(b, i, f, pool):
+        y0 = [(0, i, f) for i in range(NT) for f in range(G)]
+        rounds = []
+        turns = []
+
+        def y_front(b, i, f):
             y_matmuls(b, i, f)
-            if pool:
+            if (b, i, f) in ((0, 0, 0), (0, 0, 1), (0, 1, 0), (0, 2, 0), (0, 2, 1)):
                 y_raw_copy(b, i, f)
                 y_add_pool(b, i, f)
             else:
                 y_add(b, i, f)
 
-        y0 = [(0, i, f) for i in range(NT) for f in range(G)]
-        rounds = []
-        turns = []
+        def y_turn_pair():
+            if len(turns) >= 2:
+                pair = [turns.pop(0), turns.pop(0)]
+                for i in pair:
+                    y_transposes(0, i)
+                for i in pair:
+                    y_copy(nc.scalar, 0, i)
 
-        def y_turn():
-            i = turns.pop(0)
-            y_transposes(0, i)
-            y_copy(nc.scalar, 0, i)
+        def y_round_next():
+            b, i, f = rounds.pop(0)
+            y_round(nc.gpsimd if (b, i, f) in () else nc.scalar, b, i, f)
+            if f == 1:
+                y_store(b, i)
+                turns.append(i)
 
-        def y0_step(pool):
+        def y0_step():
             if y0:
                 b, i, f = y0.pop(0)
-                y_front(b, i, f, pool)
+                y_front(b, i, f)
                 rounds.append((b, i, f))
-            if len(rounds) > 2:
-                b, i, f = rounds.pop(0)
-                y_round(nc.scalar, b, i, f)
-                if f == 1:
-                    y_store(b, i)
-                    turns.append(i)
-            elif turns:
-                y_turn()
+            if len(rounds) > 1:
+                y_round_next()
 
         for m in range(8):
             k_matmuls(1, m)
             k_pool(1, m)
             if m == 1:
                 z_quant(0, NT - 1)
-            if m in (2, 4, 6):
-                y0_step(m in (2, 6))
+            if m in (1, 5, 7):
+                y0_step()
         cv_spread(1)
-        y0_step(True)
-        y0_step(False)
+        for k in range(1):
+            y0_step()
         cv_move(1)
         cv_pick(1)
         for i in range(NT):
             for h in range(G):
                 v_matmuls(1, i, h)
-                v_gate(1, i, h)
-                y0_step((i + h) % 2 == 0)
-                if turns and h == 1:
-                    y_turn()
-            if i > 0:
-                z_quant(1, i - 1)
-        for b, i, f in rounds:
-            y_round(nc.scalar, b, i, f)
-        y_store(0, NT - 1)
-        turns.append(NT - 1)
+                gate(1, i, h)
+                y0_step()
+                if h == 0 and i > 0:
+                    z_quant(1, i - 1)
+            if i == 2:
+                y_turn_pair()
+        while rounds:
+            y_round_next()
         z_quant(1, NT - 1)
-        for i in range(NT):
+        last = NT - 1
+        for i in range(last):
             for f in range(G):
-                y_front(1, i, f, False)
-                y_round(nc.scalar, 1, i, f)
-                if turns:
-                    y_turn()
+                y_front(1, i, f)
+                y_round(nc.gpsimd if f in (1,) else nc.scalar, 1, i, f)
             y_store(1, i)
+            if i == 0:
+                y_turn_pair()
             if i == 1:
                 y_quant(0, 0, N, 0)
-            if i == 2:
-                y_quant(0, 0, N, 1)
-                plane_store(0, 0, N)
-            if i > 0:
-                y_transposes(1, i - 1)
-                y_copy(nc.scalar, 1, i - 1)
-            if i == 3:
-                for g in range(G):
-                    y_quant(1, 0, 256, g)
-                plane_store(1, 0, 256)
-        y_transposes(1, NT - 1)
-        y_copy(nc.scalar, 1, NT - 1)
+        y_matmuls(1, last, 0)
+        y_round_from_psum(1, last, 0)
+        y_transposes(1, 0)
+        y_transposes(1, 1)
+        y_copy(nc.scalar, 1, 0)
+        y_copy(nc.scalar, 1, 1)
+        y_add_last(1, last, 0)
+        y_quant(0, 0, N, 1)
+        plane_store(nc.sync, 0, 0, N)
+        y_matmuls(1, last, 1)
+        y_round_from_psum(1, last, 1)
+        y_finish_half(nc.scalar, 1, last, 0)
+        for g in range(G):
+            y_quant(1, 0, 256, g)
+        plane_store(nc.sync, 1, 0, 256)
+        y_transposes(1, 2)
+        y_copy(nc.scalar, 1, 2)
+        y_finish_half(nc.scalar, 1, last, 1)
+        y_add_last(1, last, 1)
         for g in range(G):
             y_quant(1, 256, N, g)
-        plane_store(1, 256, N)
+        plane_store(nc.scalar, 1, 256, N)

@@ -50,6 +50,7 @@ def tile_mobilevitv2separablecontextgate_x2_kernel(
         wo_s = sb("wo_s", [P, D], U8)
         x_sb = [sb("x_sb_%d" % b, [P, NT, D], BF16) for b in range(B)]
         xt = [sb("xt_%d" % b, [P, G, N, 4], BF16) for b in range(B)]
+        xu = [sb("xu_%d" % b, [P, G, 2, N, 2], BF16) for b in range(B)]
         xq = [sb("xq_%d" % b, [P, G, N], I32) for b in range(B)]
         xs = [sb("xs_%d" % b, [P, G, N], U8) for b in range(B)]
         escore = [sb("escore_%d" % b, [P, N], F32) for b in range(B)]
@@ -64,7 +65,7 @@ def tile_mobilevitv2separablecontextgate_x2_kernel(
         zs = [sb("zs_%d" % b, [P, NT, G, P], U8) for b in range(B)]
         yt = [sb("yt_%d" % b, [P, G, N, 4], BF16) for b in range(B)]
         yq = [sb("yq_%d" % b, [P, G, N], I32) for b in range(B)]
-        ys = [sb("ys_%d" % b, [P, N], U8) for b in range(B)]
+        ys = sb("ys", [P, B * N], U8)
 
         def words(dram, g):
             return dram[g].rearrange("p n t -> p (n t)").bitcast(I32)
@@ -118,19 +119,30 @@ def tile_mobilevitv2separablecontextgate_x2_kernel(
                 nc.tensor.transpose(bank[:, k, :], xw[:, i, k, :], ident[:])
             tr_tiles[("x", 1, i)] = bank
 
-        def x_copy(engine, b, i):
-            evacuate(engine, tr_tiles.pop(("x", b, i)), xt[b], i)
-
-        def quantize_tokens(src, codes, scales, g, lo, hi, packed):
-            nc.vector.quantize_mx(
-                out=codes[:, g, lo:hi].bitcast(FP8X4),
-                scales=scales[4 * g : P, lo:hi] if packed else scales[:, g, lo:hi],
-                in_=src[:, g, lo:hi, :].rearrange("p n t -> p (n t)"),
+        def x_copy(b, i):
+            rows = slice(P * i, P * (i + 1))
+            nc.scalar.copy(
+                out=xu[b][:, :, :, rows, :].rearrange("p g u n e -> p g u (n e)").bitcast(F32),
+                in_=tr_tiles.pop(("x", b, i))[:].rearrange("p (g u) n -> p g u n", u=2),
             )
+
+        def x_interleave(engine, b, i):
+            rows = slice(P * i, P * (i + 1))
+            out = xt[b][:, :, rows, :].bitcast(F32)
+            src = xu[b][:, :, :, rows, :].rearrange("p g u n e -> p g u (n e)").bitcast(F32)
+            src = src.rearrange("p g u n -> p g n u")
+            if engine is nc.vector:
+                engine.tensor_copy(out=out, in_=src)
+            else:
+                engine.copy(out=out, in_=src)
 
         def x_quant(b, lo, hi):
             for g in range(G):
-                quantize_tokens(xt[b], xq[b], xs[b], g, lo, hi, False)
+                nc.vector.quantize_mx(
+                    out=xq[b][:, g, lo:hi].bitcast(FP8X4),
+                    scales=xs[b][:, g, lo:hi],
+                    in_=xt[b][:, g, lo:hi, :].rearrange("p n t -> p (n t)"),
+                )
 
         a_tiles = {}
 
@@ -143,7 +155,7 @@ def tile_mobilevitv2separablecontextgate_x2_kernel(
                 nc.tensor.matmul(
                     bank[:, lo:hi],
                     lhsT=wi_neg[:, g, t : t + 1].to_broadcast([P, P]),
-                    rhs=xt[b][:, g, lo:hi, t],
+                    rhs=xu[b][:, g, t // 2, lo:hi, t % 2],
                     start=(k == 0),
                     stop=(k == 7),
                 )
@@ -265,7 +277,7 @@ def tile_mobilevitv2separablecontextgate_x2_kernel(
             )
 
         def gate(b, i, h):
-            if (b, i, h) in ((0, 0, 0), (0, 2, 0), (0, 3, 1)):
+            if (b, i, h) in ():
                 v_gate_pool(b, i, h)
             else:
                 v_gate(b, i, h)
@@ -381,18 +393,23 @@ def tile_mobilevitv2separablecontextgate_x2_kernel(
             evacuate(engine, tr_tiles.pop(("y", b, i)), yt[b], i)
 
         def y_quant(b, lo, hi, g):
-            quantize_tokens(yt[b], yq[b], ys[b], g, lo, hi, True)
+            nc.vector.quantize_mx(
+                out=yq[b][:, g, lo:hi].bitcast(FP8X4),
+                scales=ys[4 * g : P, N * b + lo : N * b + hi],
+                in_=yt[b][:, g, lo:hi, :].rearrange("p n t -> p (n t)"),
+            )
 
-        def plane_store(engine, b, lo, hi):
+        def word_store(b, lo, hi):
             nc.sync.dma_start(
                 out=out_1.rearrange("g p n t -> p g (n t)").bitcast(I32)[:, :, N * b + lo : N * b + hi],
                 in_=yq[b][:, :, lo:hi],
             )
-            for q in range(4):
-                (nc.sync if q % 2 else engine).dma_start(
-                    out=out_2[:, 4 * q : 4 * q + 4, N * b + lo : N * b + hi].bitcast(I32),
-                    in_=ys[b][32 * q : 32 * q + 8, lo:hi].bitcast(I32),
-                )
+
+        def scale_store(q, engine):
+            engine.dma_start(
+                out=out_2[:, 4 * q : 4 * q + 4, :].bitcast(I32),
+                in_=ys[32 * q : 32 * q + 8, :].bitcast(I32),
+            )
 
         def permute_wv(g):
             nc.vector.tensor_copy(
@@ -415,18 +432,18 @@ def tile_mobilevitv2separablecontextgate_x2_kernel(
         for tile in (wk_s, wvs_in, wo_s):
             nc.vector.memset(tile[:].bitcast(I32), 0)
         make_identity(nc, ident[:])
-        nc.scalar.dma_start(out=wi_sb[:], in_=wi.rearrange("(g p t) -> p g t", p=P, t=4))
-        load_scales(nc.scalar, wk_s, wk_scales)
         for i in range(NT):
             load_x(0, i, i + 1)
-        load_w(wk_sb, wk_words, 0, 512)
         load_w(wv_in, wv_words, 0, D)
-        load_scales(nc.sync, wvs_in, wv_scales)
-        load_w(wk_sb, wk_words, 512, D)
+        load_w(wk_sb, wk_words, 0, 512)
+        nc.scalar.dma_start(out=wi_sb[:], in_=wi.rearrange("(g p t) -> p g t", p=P, t=4))
+        load_scales(nc.gpsimd, wk_s, wk_scales)
+        load_scales(nc.gpsimd, wvs_in, wv_scales)
+        load_scales(nc.gpsimd, wo_s, wo_scales)
         load_x(1, 0, 2)
+        load_w(wk_sb, wk_words, 512, D)
         load_x(1, 2, 4)
         load_w(wo_sb, wo_words, 0, D)
-        load_scales(nc.sync, wo_s, wo_scales)
         nc.sync.dma_start(out=bo_sb[:], in_=bo.partition_broadcast(P))
 
         nc.vector.reduce_sum(out=rsel[:], in_=ident[:].rearrange("p (j t) -> p j t", t=4), axis=AX.X)
@@ -440,30 +457,34 @@ def tile_mobilevitv2separablecontextgate_x2_kernel(
             nc.tensor.matmul(bank[:], lhsT=ident[:], rhs=ident[:], start=True, stop=True)
         for i in range(NT):
             x_transposes(0, i)
-            x_copy(nc.vector if i % 2 else nc.scalar, 0, i)
+            x_copy(0, i)
         a_matmuls(0, 0, 256)
         a_matmuls(0, 256, N)
-        x_quant(0, 0, 256)
-        for i in (2, 3):
-            x_quant(0, P * i, P * (i + 1))
-        a_softmax(0)
+        for i in range(NT):
+            x_interleave(nc.vector, 0, i)
+            if i % 2:
+                x_quant(0, P * (i - 1), P * (i + 1))
         permute_wv(0)
+        a_softmax(0)
+        permute_wv(1)
+        x_reorder(0)
+        x_reorder(1)
         for m in range(8):
             k_matmuls(0, m)
             k_pool(0, m)
             if m == 1:
-                for i in range(NT):
-                    x_reorder(i)
-            if m == 2:
-                permute_wv(1)
+                x_reorder(2)
+                x_reorder(3)
             if m == 4:
                 permute_wv_scales()
-            if m in (3, 5):
-                j = 2 * (3, 5).index(m)
+            if m in (3, 6):
+                j = 2 * (3, 6).index(m)
                 for i in (j, j + 1):
                     x_transposes_reordered(i)
                 for i in (j, j + 1):
-                    x_copy(nc.scalar, 1, i)
+                    x_copy(1, i)
+                for i in (j, j + 1):
+                    x_interleave(nc.scalar, 1, i)
         a_matmuls(1, 0, N)
         cv_spread(0)
         cv_move(0)
@@ -483,7 +504,7 @@ def tile_mobilevitv2separablecontextgate_x2_kernel(
 
         def y_front(b, i, f):
             y_matmuls(b, i, f)
-            if (b, i, f) in ((0, 0, 0), (0, 0, 1), (0, 1, 0), (0, 2, 0), (0, 2, 1)):
+            if (b, i, f) in ((0, 0, 0), (0, 0, 1), (0, 1, 0), (0, 1, 1)):
                 y_raw_copy(b, i, f)
                 y_add_pool(b, i, f)
             else:
@@ -517,7 +538,7 @@ def tile_mobilevitv2separablecontextgate_x2_kernel(
             k_pool(1, m)
             if m == 1:
                 z_quant(0, NT - 1)
-            if m in (1, 5, 7):
+            if m in (1, 3, 5, 7):
                 y0_step()
         cv_spread(1)
         for k in range(1):
@@ -531,7 +552,7 @@ def tile_mobilevitv2separablecontextgate_x2_kernel(
                 y0_step()
                 if h == 0 and i > 0:
                     z_quant(1, i - 1)
-            if i == 2:
+            if i == 3:
                 y_turn_pair()
         while rounds:
             y_round_next()
@@ -552,19 +573,21 @@ def tile_mobilevitv2separablecontextgate_x2_kernel(
         y_transposes(1, 1)
         y_copy(nc.scalar, 1, 0)
         y_copy(nc.scalar, 1, 1)
-        y_add_last(1, last, 0)
         y_quant(0, 0, N, 1)
-        plane_store(nc.sync, 0, 0, N)
+        word_store(0, 0, N)
         y_matmuls(1, last, 1)
         y_round_from_psum(1, last, 1)
+        y_add_last(1, last, 0)
         y_finish_half(nc.scalar, 1, last, 0)
         for g in range(G):
             y_quant(1, 0, 256, g)
-        plane_store(nc.sync, 1, 0, 256)
+        word_store(1, 0, 256)
         y_transposes(1, 2)
         y_copy(nc.scalar, 1, 2)
         y_finish_half(nc.scalar, 1, last, 1)
         y_add_last(1, last, 1)
         for g in range(G):
             y_quant(1, 256, N, g)
-        plane_store(nc.scalar, 1, 256, N)
+        word_store(1, 256, N)
+        for q in range(4):
+            scale_store(q, nc.sync if q % 2 else nc.scalar)

@@ -85,7 +85,7 @@ def tile_mobilevitv2separablecontextgate_x2_kernel(
         tr_tiles = {}
 
         def x_transposes(b, i):
-            if i < 2:
+            if b == 1 or i < 2:
                 bank = psum.tile([P, 4, P], F32, name="trbank", tag="tr", bufs=2)
             else:
                 bank = psum.tile([P, 4, P], F32, name="trbank", tag="mm", bufs=4)
@@ -104,20 +104,6 @@ def tile_mobilevitv2separablecontextgate_x2_kernel(
                 engine.tensor_copy(out=out, in_=src)
             else:
                 engine.copy(out=out, in_=src)
-
-        xw = sb("xw", [P, NT, 4, P], F32)
-
-        def x_reorder(i):
-            nc.scalar.copy(
-                out=xw[:, i].rearrange("n (g u) p -> n g u p", u=2),
-                in_=x_sb[1][:, i, :].bitcast(F32).rearrange("n (g p u) -> n g u p", g=2, u=2),
-            )
-
-        def x_transposes_reordered(i):
-            bank = psum.tile([P, 4, P], F32, name="trbank", tag="tr", bufs=2)
-            for k in range(4):
-                nc.tensor.transpose(bank[:, k, :], xw[:, i, k, :], ident[:])
-            tr_tiles[("x", 1, i)] = bank
 
         def x_copy(b, i):
             rows = slice(P * i, P * (i + 1))
@@ -194,6 +180,19 @@ def tile_mobilevitv2separablecontextgate_x2_kernel(
                 op0=ALU.mult,
                 op1=ALU.mult,
                 accum_out=cvraw[b][:, m : m + 1],
+            )
+
+        def k_pool_split(b, m):
+            keys = work.tile([P, N], F32, name="keys", align_bytes=64)
+            nc.scalar.copy(out=keys[:], in_=k_tiles.pop((b, m))[:])
+            product = work.tile([P, N], F32, name="product_pool", align_bytes=64)
+            nc.gpsimd.tensor_tensor(out=product[:], in0=keys[:], in1=escore[b][:], op=ALU.mult)
+            return product
+
+        def k_pool_sum(b, m, product):
+            total = work.tile([P, N], BF16, name="total", align_bytes=64)
+            nc.scalar.activation(
+                out=total[:], in_=product[:], func=ACT.Identity, accum_out=cvraw[b][:, m : m + 1]
             )
 
         sh_tiles = {}
@@ -418,7 +417,7 @@ def tile_mobilevitv2separablecontextgate_x2_kernel(
             )
 
         def permute_wv_scales():
-            nc.vector.tensor_copy(
+            nc.gpsimd.tensor_copy(
                 out=wv_s[:].rearrange("p (h t j) -> p h t j", h=2, t=4),
                 in_=wvs_in[:].rearrange("p (h j t) -> p h t j", h=2, t=4),
             )
@@ -432,17 +431,16 @@ def tile_mobilevitv2separablecontextgate_x2_kernel(
         for tile in (wk_s, wvs_in, wo_s):
             nc.vector.memset(tile[:].bitcast(I32), 0)
         make_identity(nc, ident[:])
+        nc.scalar.dma_start(out=wi_sb[:], in_=wi.rearrange("(g p t) -> p g t", p=P, t=4))
         for i in range(NT):
             load_x(0, i, i + 1)
+        load_scales(nc.scalar, wk_s, wk_scales)
         load_w(wv_in, wv_words, 0, D)
         load_w(wk_sb, wk_words, 0, 512)
-        nc.scalar.dma_start(out=wi_sb[:], in_=wi.rearrange("(g p t) -> p g t", p=P, t=4))
-        load_scales(nc.gpsimd, wk_s, wk_scales)
         load_scales(nc.gpsimd, wvs_in, wv_scales)
         load_scales(nc.gpsimd, wo_s, wo_scales)
-        load_x(1, 0, 2)
+        load_x(1, 0, 4)
         load_w(wk_sb, wk_words, 512, D)
-        load_x(1, 2, 4)
         load_w(wo_sb, wo_words, 0, D)
         nc.sync.dma_start(out=bo_sb[:], in_=bo.partition_broadcast(P))
 
@@ -467,24 +465,28 @@ def tile_mobilevitv2separablecontextgate_x2_kernel(
         permute_wv(0)
         a_softmax(0)
         permute_wv(1)
-        x_reorder(0)
-        x_reorder(1)
+        permute_wv_scales()
+        late = []
         for m in range(8):
             k_matmuls(0, m)
-            k_pool(0, m)
-            if m == 1:
-                x_reorder(2)
-                x_reorder(3)
-            if m == 4:
-                permute_wv_scales()
-            if m in (3, 6):
-                j = 2 * (3, 6).index(m)
+            if m in ():
+                late.append((m, k_pool_split(0, m)))
+            else:
+                k_pool(0, m)
+            if late and m >= late[0][0] + 3:
+                j, product = late.pop(0)
+                k_pool_sum(0, j, product)
+            if m in (3, 5):
+                j = 2 * (3, 5).index(m)
                 for i in (j, j + 1):
-                    x_transposes_reordered(i)
+                    x_transposes(1, i)
                 for i in (j, j + 1):
                     x_copy(1, i)
                 for i in (j, j + 1):
                     x_interleave(nc.scalar, 1, i)
+        while late:
+            j, product = late.pop(0)
+            k_pool_sum(0, j, product)
         a_matmuls(1, 0, N)
         cv_spread(0)
         cv_move(0)
@@ -565,16 +567,15 @@ def tile_mobilevitv2separablecontextgate_x2_kernel(
             y_store(1, i)
             if i == 0:
                 y_turn_pair()
-            if i == 1:
-                y_quant(0, 0, N, 0)
+            if i > 0:
+                y_quant(0, 0, N, i - 1)
+        word_store(0, 0, N)
         y_matmuls(1, last, 0)
         y_round_from_psum(1, last, 0)
         y_transposes(1, 0)
         y_transposes(1, 1)
         y_copy(nc.scalar, 1, 0)
         y_copy(nc.scalar, 1, 1)
-        y_quant(0, 0, N, 1)
-        word_store(0, 0, N)
         y_matmuls(1, last, 1)
         y_round_from_psum(1, last, 1)
         y_add_last(1, last, 0)

@@ -38,6 +38,8 @@ def tile_mobilevitv2separablecontextgate_x2_kernel(
         mask_t = sb("mask_t", [P, 4], F32)
         mask_q = sb("mask_q", [P, 4], F32)
         wi_sb = sb("wi_sb", [P, G, 4], BF16)
+        zero = sb("zero", [P, 1], F32)
+        one = sb("one", [P, 1], F32)
         wi_neg = sb("wi_neg", [P, G, 4], BF16)
         bo_sb = sb("bo_sb", [P, D], BF16)
         wk_sb = sb("wk_sb", [P, G, D], I32)
@@ -122,13 +124,12 @@ def tile_mobilevitv2separablecontextgate_x2_kernel(
             else:
                 engine.copy(out=out, in_=src)
 
-        def x_quant(b, lo, hi):
-            for g in range(G):
-                nc.vector.quantize_mx(
-                    out=xq[b][:, g, lo:hi].bitcast(FP8X4),
-                    scales=xs[b][:, g, lo:hi],
-                    in_=xt[b][:, g, lo:hi, :].rearrange("p n t -> p (n t)"),
-                )
+        def x_quant(b, lo, hi, g):
+            nc.vector.quantize_mx(
+                out=xq[b][:, g, lo:hi].bitcast(FP8X4),
+                scales=xs[b][:, g, lo:hi],
+                in_=xt[b][:, g, lo:hi, :].rearrange("p n t -> p (n t)"),
+            )
 
         a_tiles = {}
 
@@ -207,7 +208,7 @@ def tile_mobilevitv2separablecontextgate_x2_kernel(
             )
 
         def cv_move(b):
-            bank = psum.tile([P, 8, 4], F32, name="shbank", tag="y", bufs=2)
+            bank = psum.tile([P, 8, 4], F32, name="shbank", tag="tr", bufs=2)
             nc.tensor.matmul(
                 bank[:].rearrange("p a q -> p (a q)"),
                 lhsT=bsel[:].rearrange("p q j -> p (q j)"),
@@ -226,6 +227,8 @@ def tile_mobilevitv2separablecontextgate_x2_kernel(
                 op0=ALU.mult,
                 op1=ALU.mult,
             )
+
+        def cv_sum(b):
             nc.vector.reduce_sum(
                 out=cvz[b][:].rearrange("p t g -> p (t g)"), in_=cvpick[b][:], axis=AX.X
             )
@@ -417,7 +420,7 @@ def tile_mobilevitv2separablecontextgate_x2_kernel(
             )
 
         def permute_wv_scales():
-            nc.gpsimd.tensor_copy(
+            nc.vector.tensor_copy(
                 out=wv_s[:].rearrange("p (h t j) -> p h t j", h=2, t=4),
                 in_=wvs_in[:].rearrange("p (h j t) -> p h t j", h=2, t=4),
             )
@@ -428,12 +431,14 @@ def tile_mobilevitv2separablecontextgate_x2_kernel(
                 in_=dram.rearrange("g p n t -> p g (n t)").bitcast(I32)[:, :, lo:hi],
             )
 
+        nc.vector.memset(zero[:], 0.0)
         for tile in (wk_s, wvs_in, wo_s):
             nc.vector.memset(tile[:].bitcast(I32), 0)
         make_identity(nc, ident[:])
         nc.scalar.dma_start(out=wi_sb[:], in_=wi.rearrange("(g p t) -> p g t", p=P, t=4))
         for i in range(NT):
             load_x(0, i, i + 1)
+        nc.scalar.activation(out=one[:], in_=zero[:], func=ACT.Exp)
         load_scales(nc.scalar, wk_s, wk_scales)
         load_w(wv_in, wv_words, 0, D)
         load_w(wk_sb, wk_words, 0, 512)
@@ -447,25 +452,29 @@ def tile_mobilevitv2separablecontextgate_x2_kernel(
         nc.vector.reduce_sum(out=rsel[:], in_=ident[:].rearrange("p (j t) -> p j t", t=4), axis=AX.X)
         nc.vector.reduce_sum(out=mask_t[:], in_=ident[:].rearrange("p (j t) -> p t j", t=4), axis=AX.X)
         nc.vector.reduce_sum(out=mask_q[:], in_=ident[:].rearrange("p (q j) -> p q j", q=4), axis=AX.X)
-        nc.vector.tensor_scalar(out=wi_neg[:], in0=wi_sb[:], scalar1=-1.0, scalar2=None, op0=ALU.mult)
         nc.vector.tensor_copy(out=bsel[:], in_=rsel[:].unsqueeze(1).to_broadcast([P, 4, 32]))
 
-        for k in range(4):
+        for k in range(3):
             bank = psum.tile([P, P], F32, name="warmbank", tag="tr", bufs=2)
             nc.tensor.matmul(bank[:], lhsT=ident[:], rhs=ident[:], start=True, stop=True)
+        nc.vector.tensor_scalar(
+            out=wi_neg[:], in0=wi_sb[:], scalar1=one[:], scalar2=-1.0, op0=ALU.mult, op1=ALU.mult
+        )
         for i in range(NT):
+            if i == NT - 1:
+                a_matmuls(0, 0, P)
             x_transposes(0, i)
             x_copy(0, i)
-        a_matmuls(0, 0, 256)
-        a_matmuls(0, 256, N)
+        a_matmuls(0, P, 3 * P)
+        a_matmuls(0, 3 * P, N)
         for i in range(NT):
             x_interleave(nc.vector, 0, i)
             if i % 2:
-                x_quant(0, P * (i - 1), P * (i + 1))
+                for g in range(G):
+                    x_quant(0, P * (i - 1), P * (i + 1), g)
         permute_wv(0)
         a_softmax(0)
         permute_wv(1)
-        permute_wv_scales()
         late = []
         for m in range(8):
             k_matmuls(0, m)
@@ -473,6 +482,8 @@ def tile_mobilevitv2separablecontextgate_x2_kernel(
                 late.append((m, k_pool_split(0, m)))
             else:
                 k_pool(0, m)
+            if m == 4:
+                permute_wv_scales()
             if late and m >= late[0][0] + 3:
                 j, product = late.pop(0)
                 k_pool_sum(0, j, product)
@@ -490,8 +501,10 @@ def tile_mobilevitv2separablecontextgate_x2_kernel(
         a_matmuls(1, 0, N)
         cv_spread(0)
         cv_move(0)
-        x_quant(1, 0, N)
+        x_quant(1, 0, N, 0)
         cv_pick(0)
+        x_quant(1, 0, N, 1)
+        cv_sum(0)
         for i in range(NT):
             for h in range(G):
                 v_matmuls(0, i, h)
@@ -543,10 +556,11 @@ def tile_mobilevitv2separablecontextgate_x2_kernel(
             if m in (1, 3, 5, 7):
                 y0_step()
         cv_spread(1)
-        for k in range(1):
-            y0_step()
+        y0_step()
         cv_move(1)
         cv_pick(1)
+        y0_step()
+        cv_sum(1)
         for i in range(NT):
             for h in range(G):
                 v_matmuls(1, i, h)
@@ -563,7 +577,7 @@ def tile_mobilevitv2separablecontextgate_x2_kernel(
         for i in range(last):
             for f in range(G):
                 y_front(1, i, f)
-                y_round(nc.gpsimd if f in (1,) else nc.scalar, 1, i, f)
+                y_round(nc.gpsimd if f in () else nc.scalar, 1, i, f)
             y_store(1, i)
             if i == 0:
                 y_turn_pair()

from contextlib import ExitStack

import concourse.mybir as mybir
from concourse.masks import make_identity

F32 = mybir.dt.float32
BF16 = mybir.dt.bfloat16
I32 = mybir.dt.int32
U8 = mybir.dt.uint8
FP8X4 = mybir.dt.float8_e4m3fn_x4
ALU = mybir.AluOpType
ACT = mybir.ActivationFunctionType
AX = mybir.AxisListType

B, N, D = 2, 512, 1024
P = 128
G = 2
NT = 4
FLOPS = 3 * 2 * B * N * D * D


def tile_mobilevitv2separablecontextgate_x2_kernel(
    tc, x, wi, wk_words, wk_scales, wv_words, wv_scales, wo_words, wo_scales, bo, out_0, out_1, out_2
):
    nc = tc.nc
    with ExitStack() as ctx:
        keep = ctx.enter_context(tc.tile_pool(name="keep", bufs=1))
        work = ctx.enter_context(tc.tile_pool(name="work", bufs=3))
        psum = ctx.enter_context(tc.psum_pool(name="psum", bufs=1))
        ctx.enter_context(tc.manual_schedule())

        def sb(name, shape, dtype):
            return keep.tile(shape, dtype, name=name, align_bytes=64)

        ident = sb("ident", [P, P], F32)
        rsel = sb("rsel", [P, 32], F32)
        bsel = sb("bsel", [P, 4, 32], F32)
        mask_t = sb("mask_t", [P, 4], F32)
        mask_q = sb("mask_q", [P, 4], F32)
        wi_sb = sb("wi_sb", [P, G, 4], BF16)
        zero = sb("zero", [P, 1], F32)
        one = sb("one", [P, 1], F32)
        wi_neg = sb("wi_neg", [P, G, 4], BF16)
        bo_sb = sb("bo_sb", [P, D], BF16)
        wk_sb = sb("wk_sb", [P, G, D], I32)
        wv_in = sb("wv_in", [P, G, D], I32)
        wv_sb = sb("wv_sb", [P, G, D], I32)
        wo_sb = sb("wo_sb", [P, G, D], I32)
        wk_s = sb("wk_s", [P, D], U8)
        wvs_in = sb("wvs_in", [P, D], U8)
        wv_s = sb("wv_s", [P, D], U8)
        wo_s = sb("wo_s", [P, D], U8)
        x_sb = [sb("x_sb_%d" % b, [P, NT, D], BF16) for b in range(B)]
        xt = [sb("xt_%d" % b, [P, G, N, 4], BF16) for b in range(B)]
        xu = [sb("xu_%d" % b, [P, G, 2, N, 2], BF16) for b in range(B)]
        xq = [sb("xq_%d" % b, [P, G, N], I32) for b in range(B)]
        xs = [sb("xs_%d" % b, [P, G, N], U8) for b in range(B)]
        escore = [sb("escore_%d" % b, [P, N], F32) for b in range(B)]
        amax = [sb("amax_%d" % b, [P, 1], F32) for b in range(B)]
        esum = [sb("esum_%d" % b, [P, 1], F32) for b in range(B)]
        rsum = [sb("rsum_%d" % b, [P, 1], F32) for b in range(B)]
        cvraw = [sb("cvraw_%d" % b, [P, 8], F32) for b in range(B)]
        cvspread = [sb("cvspread_%d" % b, [P, 4, 8], F32) for b in range(B)]
        cvpick = [sb("cvpick_%d" % b, [P, 8, 4], F32) for b in range(B)]
        cvz = [sb("cvz_%d" % b, [P, 4, G], F32) for b in range(B)]
        zq = [sb("zq_%d" % b, [P, NT, G, P], I32) for b in range(B)]
        zs = [sb("zs_%d" % b, [P, NT, G, P], U8) for b in range(B)]
        yt = [sb("yt_%d" % b, [P, G, N, 4], BF16) for b in range(B)]
        yq = [sb("yq_%d" % b, [P, G, N], I32) for b in range(B)]
        ys = sb("ys", [P, B * N], U8)

        def words(dram, g):
            return dram[g].rearrange("p n t -> p (n t)").bitcast(I32)

        def load_scales(engine, tile, dram):
            for q in range(4):
                engine.dma_start(
                    out=tile[32 * q : 32 * q + 8, :].bitcast(I32),
                    in_=dram[:, 4 * q : 4 * q + 4, :].bitcast(I32),
                )

        def load_x(b, lo, hi):
            nc.sync.dma_start(
                out=x_sb[b][:, lo:hi, :], in_=x[b, P * lo : P * hi, :].rearrange("(i p) d -> p i d", p=P)
            )

        tr_tiles = {}

        def x_transposes(b, i):
            if b == 1 or i < 2:
                bank = psum.tile([P, 4, P], F32, name="trbank", tag="tr", bufs=2)
            else:
                bank = psum.tile([P, 4, P], F32, name="trbank", tag="mm", bufs=4)
            w = x_sb[b][:, i, :].bitcast(F32)
            for g in range(G):
                for u in range(2):
                    nc.tensor.transpose(
                        bank[:, 2 * g + u, :], w[:, 256 * g + u : 256 * (g + 1) : 2], ident[:]
                    )
            tr_tiles[("x", b, i)] = bank

        def evacuate(engine, bank, dst, i):
            out = dst[:, :, P * i : P * (i + 1), :].bitcast(F32)
            src = bank[:].rearrange("p (g u) r -> p g r u", u=2)
            if engine is nc.vector:
                engine.tensor_copy(out=out, in_=src)
            else:
                engine.copy(out=out, in_=src)

        def x_copy(b, i):
            rows = slice(P * i, P * (i + 1))
            nc.scalar.copy(
                out=xu[b][:, :, :, rows, :].rearrange("p g u n e -> p g u (n e)").bitcast(F32),
                in_=tr_tiles.pop(("x", b, i))[:].rearrange("p (g u) n -> p g u n", u=2),
            )

        def x_interleave(engine, b, i):
            rows = slice(P * i, P * (i + 1))
            out = xt[b][:, :, rows, :].bitcast(F32)
            src = xu[b][:, :, :, rows, :].rearrange("p g u n e -> p g u (n e)").bitcast(F32)
            src = src.rearrange("p g u n -> p g n u")
            if engine is nc.vector:
                engine.tensor_copy(out=out, in_=src)
            else:
                engine.copy(out=out, in_=src)

        def x_quant(b, lo, hi, g):
            nc.vector.quantize_mx(
                out=xq[b][:, g, lo:hi].bitcast(FP8X4),
                scales=xs[b][:, g, lo:hi],
                in_=xt[b][:, g, lo:hi, :].rearrange("p n t -> p (n t)"),
            )

        a_tiles = {}

        def a_matmuls(b, lo, hi):
            if lo == 0:
                a_tiles[b] = psum.tile([P, N], F32, name="abank", tag="y", bufs=2)
            bank = a_tiles[b]
            for k in range(8):
                g, t = divmod(k, 4)
                nc.tensor.matmul(
                    bank[:, lo:hi],
                    lhsT=wi_neg[:, g, t : t + 1].to_broadcast([P, P]),
                    rhs=xu[b][:, g, t // 2, lo:hi, t % 2],
                    start=(k == 0),
                    stop=(k == 7),
                )

        def a_softmax(b):
            bank = a_tiles.pop(b)
            nc.vector.tensor_reduce(out=amax[b][:], in_=bank[:], axis=AX.X, op=ALU.min)
            nc.scalar.activation(
                out=escore[b][:], in_=bank[:], func=ACT.Exp, bias=amax[b][:], scale=-1.0, accum_out=esum[b][:]
            )

        k_tiles = {}

        def k_matmuls(b, m):
            bank = psum.tile([P, N], F32, name="kbank", tag="mm", bufs=4)
            cols = slice(P * m, P * (m + 1))
            for g in range(G):
                nc.tensor.matmul_mx(
                    out=bank[:],
                    lhsT=wk_sb[:, g, cols].bitcast(FP8X4),
                    lhsT_scale=wk_s[4 * g : P, cols],
                    rhs=xq[b][:, g, :].bitcast(FP8X4),
                    rhs_scale=xs[b][:, g, :],
                    start=(g == 0),
                    stop=(g == 1),
                )
            k_tiles[(b, m)] = bank

        def k_pool(b, m):
            product = work.tile([P, N], BF16, name="product", align_bytes=64)
            nc.vector.scalar_tensor_tensor(
                out=product[:],
                in0=k_tiles.pop((b, m))[:],
                scalar=1.0,
                in1=escore[b][:],
                op0=ALU.mult,
                op1=ALU.mult,
                accum_out=cvraw[b][:, m : m + 1],
            )

        def k_pool_split(b, m):
            keys = work.tile([P, N], F32, name="keys", align_bytes=64)
            nc.scalar.copy(out=keys[:], in_=k_tiles.pop((b, m))[:])
            product = work.tile([P, N], F32, name="product_pool", align_bytes=64)
            nc.gpsimd.tensor_tensor(out=product[:], in0=keys[:], in1=escore[b][:], op=ALU.mult)
            return product

        def k_pool_sum(b, m, product):
            total = work.tile([P, N], BF16, name="total", align_bytes=64)
            nc.scalar.activation(
                out=total[:], in_=product[:], func=ACT.Identity, accum_out=cvraw[b][:, m : m + 1]
            )

        sh_tiles = {}

        def cv_spread(b):
            nc.vector.reciprocal(out=rsum[b][:], in_=esum[b][:])
            nc.vector.tensor_tensor(
                out=cvspread[b][:],
                in0=cvraw[b][:].unsqueeze(1).to_broadcast([P, 4, 8]),
                in1=mask_t[:].unsqueeze(2).to_broadcast([P, 4, 8]),
                op=ALU.mult,
            )

        def cv_move(b):
            bank = psum.tile([P, 8, 4], F32, name="shbank", tag="tr", bufs=2)
            nc.tensor.matmul(
                bank[:].rearrange("p a q -> p (a q)"),
                lhsT=bsel[:].rearrange("p q j -> p (q j)"),
                rhs=cvspread[b][:].rearrange("p t m -> p (t m)"),
                start=True,
                stop=True,
            )
            sh_tiles[b] = bank

        def cv_pick(b):
            nc.vector.scalar_tensor_tensor(
                out=cvpick[b][:],
                in0=sh_tiles.pop(b)[:],
                scalar=rsum[b][:],
                in1=mask_q[:].unsqueeze(1).to_broadcast([P, 8, 4]),
                op0=ALU.mult,
                op1=ALU.mult,
            )

        def cv_sum(b):
            nc.vector.reduce_sum(
                out=cvz[b][:].rearrange("p t g -> p (t g)"), in_=cvpick[b][:], axis=AX.X
            )

        v_tiles = {}
        z_tiles = {}

        def v_matmuls(b, i, h):
            bank = psum.tile([P, 4, P], F32, name="vbank", tag="mm", bufs=4)
            for t in range(4):
                cols = slice(512 * h + P * t, 512 * h + P * (t + 1))
                for g in range(G):
                    nc.tensor.matmul_mx(
                        out=bank[:, t, :],
                        lhsT=wv_sb[:, g, cols].bitcast(FP8X4),
                        lhsT_scale=wv_s[4 * g : P, cols],
                        rhs=xq[b][:, g, P * i : P * (i + 1)].bitcast(FP8X4),
                        rhs_scale=xs[b][:, g, P * i : P * (i + 1)],
                        start=(g == 0),
                        stop=(g == 1),
                    )
            v_tiles[(b, i, h)] = bank

        def v_gate(b, i, h):
            if h == 0:
                z_tiles[(b, i)] = work.tile([P, G, P, 4], BF16, name="z", align_bytes=64)
            nc.vector.scalar_tensor_tensor(
                out=z_tiles[(b, i)][:, h],
                in0=v_tiles.pop((b, i, h))[:].rearrange("p t n -> p n t"),
                scalar=0.0,
                in1=cvz[b][:, :, h].unsqueeze(1).to_broadcast([P, P, 4]),
                op0=ALU.max,
                op1=ALU.mult,
            )

        def v_gate_pool(b, i, h):
            if h == 0:
                z_tiles[(b, i)] = work.tile([P, G, P, 4], BF16, name="z", align_bytes=64)
            vrelu = work.tile([P, P, 4], F32, name="vrelu", align_bytes=64)
            nc.scalar.activation(
                out=vrelu[:], in_=v_tiles.pop((b, i, h))[:].rearrange("p t n -> p n t"), func=ACT.Relu
            )
            nc.gpsimd.tensor_tensor(
                out=z_tiles[(b, i)][:, h],
                in0=vrelu[:],
                in1=cvz[b][:, :, h].unsqueeze(1).to_broadcast([P, P, 4]),
                op=ALU.mult,
            )

        def gate(b, i, h):
            if (b, i, h) in ():
                v_gate_pool(b, i, h)
            else:
                v_gate(b, i, h)

        def z_quant(b, i):
            nc.vector.quantize_mx(
                out=zq[b][:, i].rearrange("p g n -> p (g n)").bitcast(FP8X4),
                scales=zs[b][:, i].rearrange("p g n -> p (g n)"),
                in_=z_tiles.pop((b, i))[:].rearrange("p g n t -> p (g n t)"),
            )

        y_banks = {}
        y_rows = {}
        y_half = {}

        def y_matmuls(b, i, f):
            if b == 0:
                bank = psum.tile([P, 512], F32, name="ybank", tag="y", bufs=2)
            else:
                bank = psum.tile([P, 512], F32, name="ybank", tag="mm", bufs=4)
            cols = slice(512 * f, 512 * (f + 1))
            for g in range(G):
                nc.tensor.matmul_mx(
                    out=bank[:],
                    lhsT=zq[b][:, i, g, :].bitcast(FP8X4),
                    lhsT_scale=zs[b][:, i, g, :],
                    rhs=wo_sb[:, g, cols].bitcast(FP8X4),
                    rhs_scale=wo_s[4 * g : P, cols],
                    start=(g == 0),
                    stop=(g == 1),
                )
            y_banks[(b, i, f)] = bank

        def y_add(b, i, f):
            if f == 0:
                y_rows[(b, i)] = work.tile([P, D], F32, name="yrow", align_bytes=64)
            cols = slice(512 * f, 512 * (f + 1))
            nc.vector.tensor_tensor(
                out=y_rows[(b, i)][:, cols], in0=y_banks.pop((b, i, f))[:], in1=bo_sb[:, cols], op=ALU.add
            )

        y_raw = {}

        def y_raw_copy(b, i, f):
            y_raw[(b, i, f)] = work.tile([P, 512], F32, name="yraw", align_bytes=64)
            nc.scalar.copy(out=y_raw[(b, i, f)][:], in_=y_banks.pop((b, i, f))[:])

        def y_add_pool(b, i, f):
            if f == 0:
                y_rows[(b, i)] = work.tile([P, D], F32, name="yrow", align_bytes=64)
            cols = slice(512 * f, 512 * (f + 1))
            nc.gpsimd.tensor_tensor(
                out=y_rows[(b, i)][:, cols], in0=y_raw.pop((b, i, f))[:], in1=bo_sb[:, cols], op=ALU.add
            )

        def y_store(b, i):
            nc.sync.dma_start(out=out_0[b, P * i : P * (i + 1), :], in_=y_rows[(b, i)][:])

        def y_round(engine, b, i, f):
            if f == 0:
                y_half[(b, i)] = work.tile([P, G, 2, P, 2], BF16, name="yhalf", align_bytes=64)
            src = y_rows[(b, i)][:, 512 * f : 512 * (f + 1)].rearrange("n (p u e) -> n u p e", u=2, e=2)
            if engine is nc.gpsimd:
                engine.tensor_scalar(
                    out=y_half[(b, i)][:, f], in0=src, scalar1=1.0, scalar2=0.0, op0=ALU.mult, op1=ALU.add
                )
            elif engine is nc.vector:
                engine.tensor_copy(out=y_half[(b, i)][:, f], in_=src)
            else:
                engine.copy(out=y_half[(b, i)][:, f], in_=src)

        def y_transposes(b, i):
            bank = psum.tile([P, 4, P], F32, name="trbank", tag="tr", bufs=2)
            w = y_half.pop((b, i))[:].rearrange("n g u p e -> n (g u p e)").bitcast(F32)
            for k in range(4):
                nc.tensor.transpose(bank[:, k, :], w[:, P * k : P * (k + 1)], ident[:])
            tr_tiles[("y", b, i)] = bank

        def y_round_from_psum(b, i, f):
            if f == 0:
                y_half[(b, i)] = work.tile([P, G, 2, P, 2], BF16, name="yhalf", align_bytes=64)
                y_rows[(b, i)] = work.tile([P, D], F32, name="yrow", align_bytes=64)
            pairs = "n (p u e) -> n u p e"
            cols = slice(512 * f, 512 * (f + 1))
            nc.vector.tensor_tensor(
                out=y_half[(b, i)][:, f],
                in0=y_banks[(b, i, f)][:].rearrange(pairs, u=2, e=2),
                in1=bo_sb[:, cols].rearrange(pairs, u=2, e=2),
                op=ALU.add,
            )

        def y_add_last(b, i, f):
            cols = slice(512 * f, 512 * (f + 1))
            nc.vector.tensor_tensor(
                out=y_rows[(b, i)][:, cols], in0=y_banks.pop((b, i, f))[:], in1=bo_sb[:, cols], op=ALU.add
            )
            nc.sync.dma_start(out=out_0[b, P * i : P * (i + 1), cols], in_=y_rows[(b, i)][:, cols])

        def y_finish_half(engine, b, i, f):
            bank = psum.tile([P, 2, P], F32, name="trbank", tag="tr", bufs=2)
            w = y_half[(b, i)][:, f].rearrange("n u p e -> n (u p e)").bitcast(F32)
            for u in range(2):
                nc.tensor.transpose(bank[:, u, :], w[:, P * u : P * (u + 1)], ident[:])
            out = yt[b][:, f, P * i : P * (i + 1), :].rearrange("p n t -> p (n t)").bitcast(F32)
            out = out.rearrange("p (n u) -> p n u", u=2)
            src = bank[:].rearrange("p u r -> p r u")
            if engine is nc.vector:
                engine.tensor_copy(out=out, in_=src)
            else:
                engine.copy(out=out, in_=src)

        def y_copy(engine, b, i):
            evacuate(engine, tr_tiles.pop(("y", b, i)), yt[b], i)

        def y_quant(b, lo, hi, g):
            nc.vector.quantize_mx(
                out=yq[b][:, g, lo:hi].bitcast(FP8X4),
                scales=ys[4 * g : P, N * b + lo : N * b + hi],
                in_=yt[b][:, g, lo:hi, :].rearrange("p n t -> p (n t)"),
            )

        def word_store(b, lo, hi):
            nc.sync.dma_start(
                out=out_1.rearrange("g p n t -> p g (n t)").bitcast(I32)[:, :, N * b + lo : N * b + hi],
                in_=yq[b][:, :, lo:hi],
            )

        def scale_store(q, engine):
            engine.dma_start(
                out=out_2[:, 4 * q : 4 * q + 4, :].bitcast(I32),
                in_=ys[32 * q : 32 * q + 8, :].bitcast(I32),
            )

        def permute_wv(g):
            nc.vector.tensor_copy(
                out=wv_sb[:, g, :].rearrange("p (h t j) -> p h t j", h=2, t=4),
                in_=wv_in[:, g, :].rearrange("p (h j t) -> p h t j", h=2, t=4),
            )

        def permute_wv_scales():
            nc.vector.tensor_copy(
                out=wv_s[:].rearrange("p (h t j) -> p h t j", h=2, t=4),
                in_=wvs_in[:].rearrange("p (h j t) -> p h t j", h=2, t=4),
            )

        def load_w(tile, dram, lo, hi):
            nc.sync.dma_start(
                out=tile[:, :, lo:hi],
                in_=dram.rearrange("g p n t -> p g (n t)").bitcast(I32)[:, :, lo:hi],
            )

        nc.vector.memset(zero[:], 0.0)
        for tile in (wk_s, wvs_in, wo_s):
            nc.vector.memset(tile[:].bitcast(I32), 0)
        make_identity(nc, ident[:])
        nc.scalar.dma_start(out=wi_sb[:], in_=wi.rearrange("(g p t) -> p g t", p=P, t=4))
        for i in range(NT):
            load_x(0, i, i + 1)
        nc.scalar.activation(out=one[:], in_=zero[:], func=ACT.Exp)
        load_scales(nc.scalar, wk_s, wk_scales)
        load_w(wv_in, wv_words, 0, D)
        load_w(wk_sb, wk_words, 0, 512)
        load_scales(nc.gpsimd, wvs_in, wv_scales)
        load_scales(nc.gpsimd, wo_s, wo_scales)
        load_x(1, 0, 4)
        load_w(wk_sb, wk_words, 512, D)
        load_w(wo_sb, wo_words, 0, D)
        nc.sync.dma_start(out=bo_sb[:], in_=bo.partition_broadcast(P))

        nc.vector.reduce_sum(out=rsel[:], in_=ident[:].rearrange("p (j t) -> p j t", t=4), axis=AX.X)
        nc.vector.reduce_sum(out=mask_t[:], in_=ident[:].rearrange("p (j t) -> p t j", t=4), axis=AX.X)
        nc.vector.reduce_sum(out=mask_q[:], in_=ident[:].rearrange("p (q j) -> p q j", q=4), axis=AX.X)
        nc.vector.tensor_copy(out=bsel[:], in_=rsel[:].unsqueeze(1).to_broadcast([P, 4, 32]))

        for k in range(3):
            bank = psum.tile([P, P], F32, name="warmbank", tag="tr", bufs=2)
            nc.tensor.matmul(bank[:], lhsT=ident[:], rhs=ident[:], start=True, stop=True)
        nc.vector.tensor_scalar(
            out=wi_neg[:], in0=wi_sb[:], scalar1=one[:], scalar2=-1.0, op0=ALU.mult, op1=ALU.mult
        )
        for i in range(NT):
            if i == NT - 1:
                a_matmuls(0, 0, P)
            x_transposes(0, i)
            x_copy(0, i)
        a_matmuls(0, P, 3 * P)
        a_matmuls(0, 3 * P, N)
        for i in range(NT):
            x_interleave(nc.vector, 0, i)
            if i % 2:
                for g in range(G):
                    x_quant(0, P * (i - 1), P * (i + 1), g)
        permute_wv(0)
        a_softmax(0)
        permute_wv(1)
        late = []
        for m in range(8):
            k_matmuls(0, m)
            if m in ():
                late.append((m, k_pool_split(0, m)))
            else:
                k_pool(0, m)
            if m == 4:
                permute_wv_scales()
            if late and m >= late[0][0] + 3:
                j, product = late.pop(0)
                k_pool_sum(0, j, product)
            if m in (3, 5):
                j = 2 * (3, 5).index(m)
                for i in (j, j + 1):
                    x_transposes(1, i)
                for i in (j, j + 1):
                    x_copy(1, i)
                for i in (j, j + 1):
                    x_interleave(nc.scalar, 1, i)
        while late:
            j, product = late.pop(0)
            k_pool_sum(0, j, product)
        a_matmuls(1, 0, N)
        cv_spread(0)
        cv_move(0)
        x_quant(1, 0, N, 0)
        cv_pick(0)
        x_quant(1, 0, N, 1)
        cv_sum(0)
        for i in range(NT):
            for h in range(G):
                v_matmuls(0, i, h)
                gate(0, i, h)
                if i == 0 and h == 0:
                    a_softmax(1)
            if i > 0:
                z_quant(0, i - 1)
        y0 = [(0, i, f) for i in range(NT) for f in range(G)]
        rounds = []
        turns = []

        def y_front(b, i, f):
            y_matmuls(b, i, f)
            if (b, i, f) in ((0, 0, 0), (0, 0, 1), (0, 1, 0), (0, 1, 1)):
                y_raw_copy(b, i, f)
                y_add_pool(b, i, f)
            else:
                y_add(b, i, f)

        def y_turn_pair():
            if len(turns) >= 2:
                pair = [turns.pop(0), turns.pop(0)]
                for i in pair:
                    y_transposes(0, i)
                for i in pair:
                    y_copy(nc.scalar, 0, i)

        def y_round_next():
            b, i, f = rounds.pop(0)
            y_round(nc.gpsimd if (b, i, f) in () else nc.scalar, b, i, f)
            if f == 1:
                y_store(b, i)
                turns.append(i)

        def y0_step():
            if y0:
                b, i, f = y0.pop(0)
                y_front(b, i, f)
                rounds.append((b, i, f))
            if len(rounds) > 1:
                y_round_next()

        for m in range(8):
            k_matmuls(1, m)
            k_pool(1, m)
            if m == 1:
                z_quant(0, NT - 1)
            if m in (1, 3, 5, 7):
                y0_step()
        cv_spread(1)
        y0_step()
        cv_move(1)
        cv_pick(1)
        y0_step()
        cv_sum(1)
        for i in range(NT):
            for h in range(G):
                v_matmuls(1, i, h)
                gate(1, i, h)
                y0_step()
                if h == 0 and i > 0:
                    z_quant(1, i - 1)
            if i == 3:
                y_turn_pair()
        while rounds:
            y_round_next()
        z_quant(1, NT - 1)
        last = NT - 1
        for i in range(last):
            for f in range(G):
                y_front(1, i, f)
                y_round(nc.gpsimd if f in () else nc.scalar, 1, i, f)
            y_store(1, i)
            if i == 0:
                y_turn_pair()
            if i > 0:
                y_quant(0, 0, N, i - 1)
        word_store(0, 0, N)
        y_matmuls(1, last, 0)
        y_round_from_psum(1, last, 0)
        y_transposes(1, 0)
        y_transposes(1, 1)
        y_copy(nc.scalar, 1, 0)
        y_copy(nc.scalar, 1, 1)
        y_matmuls(1, last, 1)
        y_round_from_psum(1, last, 1)
        y_add_last(1, last, 0)
        y_finish_half(nc.scalar, 1, last, 0)
        for g in range(G):
            y_quant(1, 0, 256, g)
        word_store(1, 0, 256)
        y_transposes(1, 2)
        y_copy(nc.scalar, 1, 2)
        y_finish_half(nc.scalar, 1, last, 1)
        y_add_last(1, last, 1)
        for g in range(G):
            y_quant(1, 256, N, g)
        word_store(1, 256, N)
        for q in range(4):
            scale_store(q, nc.sync if q % 2 else nc.scalar)
